import numpy as np
import ml_dtypes

BF16 = ml_dtypes.bfloat16


def bf(x):
    return np.asarray(x, np.float32).astype(BF16)


def f32(x):
    return np.asarray(x, np.float32)


def f64(x):
    return np.asarray(x).astype(np.float64)


def striped(idx):
    return np.tile(idx.reshape(-1, 16).T, (8, 1))


S, K, H, M, N, D, V = 2048, 128, 128, 256, 768, 2, 384


def gelu_tanh(v):
    return 0.5 * v * (1.0 + np.tanh(np.sqrt(2.0 / np.pi) * (v + 0.044715 * v**3)))


def setup_inputs():
    return {"x": bf(np.random.standard_normal((K, S))), "w": bf(np.random.standard_normal((K, H)) / np.sqrt(K)), "b": f32(0.5 * np.random.standard_normal((H, 1))), "w2": bf(np.random.standard_normal((H, M)) / np.sqrt(D * H)), "offs": striped(np.random.permutation(S)[:N])}


def reference(x, w, b, w2, offs):
    idx = offs[:16].T.reshape(-1)
    t = gelu_tanh(f64(w).T @ f64(x) + f64(b))
    return f64(w2).T @ sum(t[:, idx[i * V : (i + 1) * V]] for i in range(D))

@@ -1,0 +1,51 @@
+import concourse.mybir as mybir
+
+BF16, F32, U16 = mybir.dt.bfloat16, mybir.dt.float32, mybir.dt.uint16
+GELU = mybir.ActivationFunctionType.Gelu_apprx_tanh
+
+P = 128
+BANK = 512
+GROUP = 16
+
+S, K, H, M, V, D = 2048, 128, 128, 256, 384, 2
+FLOPS = 2 * K * H * S + 2 * H * M * V * D
+
+
+def tile_rows_gcn2_gelu_sum_kernel(tc, x, w, b, w2, offs, out):
+    nc = tc.nc
+    with (
+        tc.tile_pool(name="held", bufs=1) as held,
+        tc.tile_pool(name="nodes", bufs=S // BANK) as nodes,
+        tc.tile_pool(name="staging", bufs=M // P) as staging,
+        tc.psum_pool(name="layer1", bufs=S // BANK) as layer1,
+        tc.psum_pool(name="layer2", bufs=M // P) as layer2,
+    ):
+        w_sb = held.tile([K, H], BF16)
+        b_sb = held.tile([H, 1], F32)
+        w2_sb = held.tile([H, M], BF16)
+        offsets = held.tile([P, D * V // GROUP], U16)
+        h = held.tile([H, S], BF16)
+
+        nc.sync.dma_start(w_sb[:], w)
+        nc.scalar.dma_start(b_sb[:], b)
+
+        for first in range(0, S, BANK):
+            x_sb = nodes.tile([K, BANK], BF16)
+            nc.sync.dma_start(x_sb[:], x[:, first : first + BANK])
+            pre = layer1.tile([H, BANK], F32)
+            nc.tensor.matmul(pre[:], w_sb[:], x_sb[:], start=True, stop=True)
+            nc.scalar.activation(h[:, first : first + BANK], pre[:], GELU, bias=b_sb[:])
+
+        nc.sync.dma_start(w2_sb[:], w2)
+        nc.sync.dma_start(offsets[:], offs)
+
+        for block in range(M // P):
+            total = layer2.tile([P, V], F32)
+            for t in range(D):
+                neighbour = offsets[:, t * V // GROUP : (t + 1) * V // GROUP]
+                nc.tensor.matmul(
+                    total[:], w2_sb[:, block * P : (block + 1) * P], h[:].indirect(neighbour), start=t == 0, stop=t == D - 1
+                )
+            result = staging.tile([P, V], F32)
+            nc.vector.tensor_copy(result[:], total[:])
+            nc.sync.dma_start(out[block * P : (block + 1) * P, :], result[:])

@@ -29,6 +29,10 @@ def tile_rows_gcn2_gelu_sum_kernel(tc, x, w, b, w2, offs, out):
         nc.sync.dma_start(w_sb[:], w)
         nc.scalar.dma_start(b_sb[:], b)
 
+        warm = held.tile([P, 1], F32)
+        nc.vector.memset(warm[:], 0.0)
+        nc.scalar.activation(warm[:], warm[:], GELU)
+
         for first in range(0, S, BANK):
             x_sb = nodes.tile([K, BANK], BF16)
             nc.sync.dma_start(x_sb[:], x[:, first : first + BANK])

@@ -15,33 +15,32 @@ def tile_rows_gcn2_gelu_sum_kernel(tc, x, w, b, w2, offs, out):
     nc = tc.nc
     with (
         tc.tile_pool(name="held", bufs=1) as held,
-        tc.tile_pool(name="nodes", bufs=S // BANK) as nodes,
-        tc.tile_pool(name="staging", bufs=M // P) as staging,
         tc.psum_pool(name="layer1", bufs=S // BANK) as layer1,
         tc.psum_pool(name="layer2", bufs=M // P) as layer2,
     ):
+        x_sb = held.tile([K, S], BF16)
         w_sb = held.tile([K, H], BF16)
         b_sb = held.tile([H, 1], F32)
         w2_sb = held.tile([H, M], BF16)
         offsets = held.tile([P, D * V // GROUP], U16)
         h = held.tile([H, S], BF16)
+        result = held.tile([P, M // P, V], F32)
 
-        nc.sync.dma_start(w_sb[:], w)
+        for first, last in ((0, BANK), (BANK, S // 2), (S // 2, S)):
+            nc.sync.dma_start(x_sb[:, first:last], x[:, first:last])
+        nc.scalar.dma_start(w_sb[:], w)
         nc.scalar.dma_start(b_sb[:], b)
+        nc.sync.dma_start(w2_sb[:], w2)
+        nc.sync.dma_start(offsets[:], offs)
 
         warm = held.tile([P, 1], F32)
         nc.vector.memset(warm[:], 0.0)
         nc.scalar.activation(warm[:], warm[:], GELU)
 
         for first in range(0, S, BANK):
-            x_sb = nodes.tile([K, BANK], BF16)
-            nc.sync.dma_start(x_sb[:], x[:, first : first + BANK])
             pre = layer1.tile([H, BANK], F32)
-            nc.tensor.matmul(pre[:], w_sb[:], x_sb[:], start=True, stop=True)
+            nc.tensor.matmul(pre[:], w_sb[:], x_sb[:, first : first + BANK], start=True, stop=True)
             nc.scalar.activation(h[:, first : first + BANK], pre[:], GELU, bias=b_sb[:])
-
-        nc.sync.dma_start(w2_sb[:], w2)
-        nc.sync.dma_start(offsets[:], offs)
 
         for block in range(M // P):
             total = layer2.tile([P, V], F32)
@@ -50,6 +49,6 @@ def tile_rows_gcn2_gelu_sum_kernel(tc, x, w, b, w2, offs, out):
                 nc.tensor.matmul(
                     total[:], w2_sb[:, block * P : (block + 1) * P], h[:].indirect(neighbour), start=t == 0, stop=t == D - 1
                 )
-            result = staging.tile([P, V], F32)
-            nc.vector.tensor_copy(result[:], total[:])
-            nc.sync.dma_start(out[block * P : (block + 1) * P, :], result[:])
+            for half in (slice(0, V // 2), slice(V // 2, V)):
+                nc.vector.tensor_copy(result[:, block, half], total[:, half])
+                nc.sync.dma_start(out[block * P : (block + 1) * P, half], result[:, block, half])

import concourse.mybir as mybir

BF16, F32, U16 = mybir.dt.bfloat16, mybir.dt.float32, mybir.dt.uint16
GELU = mybir.ActivationFunctionType.Gelu_apprx_tanh

P = 128
BANK = 512
GROUP = 16

S, K, H, M, V, D = 2048, 128, 128, 256, 384, 2
FLOPS = 2 * K * H * S + 2 * H * M * V * D


def tile_rows_gcn2_gelu_sum_kernel(tc, x, w, b, w2, offs, out):
    nc = tc.nc
    with (
        tc.tile_pool(name="held", bufs=1) as held,
        tc.psum_pool(name="layer1", bufs=S // BANK) as layer1,
        tc.psum_pool(name="layer2", bufs=M // P) as layer2,
    ):
        x_sb = held.tile([K, S], BF16)
        w_sb = held.tile([K, H], BF16)
        b_sb = held.tile([H, 1], F32)
        w2_sb = held.tile([H, M], BF16)
        offsets = held.tile([P, D * V // GROUP], U16)
        h = held.tile([H, S], BF16)
        result = held.tile([P, M // P, V], F32)

        for first, last in ((0, BANK), (BANK, S // 2), (S // 2, S)):
            nc.sync.dma_start(x_sb[:, first:last], x[:, first:last])
        nc.scalar.dma_start(w_sb[:], w)
        nc.scalar.dma_start(b_sb[:], b)
        nc.sync.dma_start(w2_sb[:], w2)
        nc.sync.dma_start(offsets[:], offs)

        warm = held.tile([P, 1], F32)
        nc.vector.memset(warm[:], 0.0)
        nc.scalar.activation(warm[:], warm[:], GELU)

        for first in range(0, S, BANK):
            pre = layer1.tile([H, BANK], F32)
            nc.tensor.matmul(pre[:], w_sb[:], x_sb[:, first : first + BANK], start=True, stop=True)
            nc.scalar.activation(h[:, first : first + BANK], pre[:], GELU, bias=b_sb[:])

        for block in range(M // P):
            total = layer2.tile([P, V], F32)
            for t in range(D):
                neighbour = offsets[:, t * V // GROUP : (t + 1) * V // GROUP]
                nc.tensor.matmul(
                    total[:], w2_sb[:, block * P : (block + 1) * P], h[:].indirect(neighbour), start=t == 0, stop=t == D - 1
                )
            for half in (slice(0, V // 2), slice(V // 2, V)):
                nc.vector.tensor_copy(result[:, block, half], total[:, half])
                nc.sync.dma_start(out[block * P : (block + 1) * P, half], result[:, block, half])
